import numpy as np
import ml_dtypes


def mxq(x, axis, fmt="e4m3"):
    dtype, down = {"e4m3": (ml_dtypes.float8_e4m3fn, 7), "e5m2": (ml_dtypes.float8_e5m2, 14)}[fmt]
    v = np.moveaxis(np.asarray(x, np.float32).astype(ml_dtypes.bfloat16).astype(np.float64), axis, -1)
    blocks = v.reshape(v.shape[:-1] + (-1, 32))
    amax = np.abs(blocks).max(-1, keepdims=True)
    byte = np.maximum(np.where(amax > 0, np.frexp(amax)[1] - 1 + 127, 0) - down, 1)
    scale = np.exp2(byte - 127.0)
    codes = (blocks / scale).astype(np.float32).astype(dtype).astype(np.float64)
    return np.moveaxis((codes * scale).reshape(v.shape), -1, axis)


WIDE = False


def mx_kscale(k):
    if not WIDE:
        return np.ones(k)
    levels = np.array([30, -30])
    if k % 512:
        return np.exp2(np.random.permutation(np.resize(levels, k // 32))).repeat(32)
    a = np.empty((k // 512, 16))
    for p in range(k // 512):
        a[p, :8] = np.random.permutation(np.resize(levels, 8))
        for g in range(8):
            far = levels[np.abs(levels - a[p, g]) >= 10]
            a[p, g + 8] = far[np.random.randint(len(far))]
    return np.exp2(a.ravel()).repeat(32)


def f64(x):
    return np.asarray(x).astype(np.float64)


def striped(idx):
    return np.tile(np.asarray(idx).reshape(-1, 16).T, (8, 1)).astype(np.uint16)


def unstriped(offs):
    return offs[:16].T.reshape(-1).astype(np.int64)


K, J, N, T, V = 256, 1024, 256, 2048, 2048


def setup_inputs():
    n = np.random.standard_normal
    idx = np.random.permutation(T)[:J]
    idx2 = np.random.permutation(V)[:J]
    fj = mx_kscale(J)
    return {
        "xf": (n((K, T))).astype(np.float32),
        "ra": (np.random.uniform(0.5, 1.5, (1, J)) * fj).astype(np.float32),
        "lo": (np.random.uniform(-0.3, 0.5, (K, 1))).astype(np.float32),
        "gt": (n((N, V)) * np.exp(0.5 * n((1, V)))).astype(np.float32),
        "rb": (np.random.uniform(0.5, 1.5, (1, J)) / fj).astype(np.float32),
        "sv": (n((N, V))).astype(np.float32),
        "gk": (np.random.uniform(0.5, 2.0, (K, 1))).astype(np.float32),
        "bn": (np.random.uniform(-12.0, 12.0, (1, N))).astype(np.float32),
        "offs": striped(idx),
        "offs2": striped(idx2),
    }


def reference(xf, ra, lo, gt, rb, sv, gk, bn, offs, offs2):
    idx = unstriped(offs)
    idx2 = unstriped(offs2)
    us = np.maximum(f64(xf)[:, idx] - f64(lo), 0.0) * f64(ra)
    uj = us.T
    gs = f64(gt)[:, idx2] * np.maximum(f64(sv)[:, idx2], 0.0) * f64(rb)
    gj = gs.T
    ujq = mxq(uj, 0, "e4m3")
    gjq = mxq(gj, 0, "e5m2")
    w = ujq.T @ gjq
    wb = w + f64(bn)
    mn = np.mean(wb, axis=1, keepdims=True)
    dw = wb - mn
    y = dw / (np.mean(np.abs(dw), axis=1, keepdims=True) + 2.0) * f64(gk)
    return y

@@ -1,0 +1,206 @@
+from contextlib import ExitStack
+
+import concourse.mybir as mybir
+from concourse.masks import make_identity
+
+K, J, N, T = 256, 1024, 256, 2048
+FLOPS = 2 * K * J * N
+
+F32 = mybir.dt.float32
+BF16 = mybir.dt.bfloat16
+U32 = mybir.dt.uint32
+U16 = mybir.dt.uint16
+U8 = mybir.dt.uint8
+E4M3 = mybir.dt.float8_e4m3fn_x4
+E5M2 = mybir.dt.float8_e5m2_x4
+ALU = mybir.AluOpType
+ACT = mybir.ActivationFunctionType
+
+P = 128
+PASS = 512
+PASSES = J // PASS
+BLOCKS = K // P
+LIST_COLS = PASS // 16
+
+
+def tile_list_moment_over_saved_spread_kernel(tc, xf, ra, lo, gt, rb, sv, gk, bn, offs, offs2, out):
+    nc = tc.nc
+    with ExitStack() as ctx:
+        keep = ctx.enter_context(tc.tile_pool(name="keep", bufs=1))
+        turn = ctx.enter_context(tc.psum_pool(name="turn", bufs=6))
+        sums = ctx.enter_context(tc.psum_pool(name="sums", bufs=1))
+
+        def sb(name, shape, dtype=F32):
+            return keep.tile(shape, dtype, name=name, align_bytes=64)
+
+        list_x = keep.tile([P, J // 16], U16, name="list_x")
+        list_g = keep.tile([P, J // 16], U16, name="list_g")
+        x_tab = [sb("x_tab%d" % b, [P, T]) for b in range(BLOCKS)]
+        g_tab = [sb("g_tab%d" % b, [P, T]) for b in range(BLOCKS)]
+        s_tab = [sb("s_tab%d" % b, [P, T]) for b in range(BLOCKS)]
+        rb_cols = sb("rb_cols", [P, J // P])
+        ra_cols = sb("ra_cols", [P, J // P])
+        bn_cols = sb("bn_cols", [P, N // P])
+        lo_cols = sb("lo_cols", [P, BLOCKS])
+        gk_cols = sb("gk_cols", [P, BLOCKS])
+
+        x_rows = xf.rearrange("(p b) t -> b p t", b=BLOCKS)
+        out_rows = out.rearrange("(p b) n -> b p n", b=BLOCKS)
+
+        nc.sync.dma_start(rb_cols[:], rb.rearrange("o (p c) -> (o p) c", p=P))
+        nc.sync.dma_start(list_g[:], offs2)
+        nc.sync.dma_start(g_tab[0][:], gt[0:P, :])
+        nc.sync.dma_start(ra_cols[:], ra.rearrange("o (p c) -> (o p) c", p=P))
+        nc.sync.dma_start(lo_cols[:], lo.rearrange("(p b) o -> p (b o)", b=BLOCKS))
+        nc.sync.dma_start(s_tab[0][:], sv[0:P, :])
+        nc.sync.dma_start(list_x[:], offs)
+        nc.sync.dma_start(x_tab[0][:], x_rows[0])
+        nc.sync.dma_start(bn_cols[:], bn.rearrange("o (p c) -> (o p) c", p=P))
+        nc.sync.dma_start(gk_cols[:], gk.rearrange("(p b) o -> p (b o)", b=BLOCKS))
+        nc.sync.dma_start(g_tab[1][:], gt[P:2 * P, :])
+        nc.sync.dma_start(s_tab[1][:], sv[P:2 * P, :])
+        nc.sync.dma_start(x_tab[1][:], x_rows[1])
+
+        ident = sb("ident", [P, P])
+        make_identity(nc, ident[:])
+
+        def spread(name, cols, count):
+            row = sb(name, [P, P * count])
+            row_v = row[:].rearrange("m (p c) -> m p c", c=count)
+            for c0 in range(0, count, 4):
+                width = min(4, count - c0)
+                bank = turn.tile([P, width, P], F32, name="turn_bank", tag="turn")
+                for c in range(width):
+                    nc.tensor.transpose(bank[:, c, :], cols[:, c0 + c:c0 + c + 1].to_broadcast([P, P]), ident[:])
+                nc.scalar.copy(row_v[:, :, c0:c0 + width], bank[:].rearrange("m c p -> m p c"))
+            return row
+
+        rb_row = spread("rb_row", rb_cols, J // P)
+        ra_row = spread("ra_row", ra_cols, J // P)
+        bn_row = spread("bn_row", bn_cols, N // P)
+
+        neg_lo = sb("neg_lo", [P, BLOCKS])
+        nc.vector.tensor_scalar(neg_lo[:], lo_cols[:], -1.0, None, ALU.mult)
+        gk_scaled = sb("gk_scaled", [P, BLOCKS])
+        nc.vector.tensor_scalar(gk_scaled[:], gk_cols[:], 1.0 / N, None, ALU.mult)
+        lo_wide = [sb("lo_wide%d" % b, [P, PASS]) for b in range(BLOCKS)]
+        for b in range(BLOCKS):
+            nc.vector.tensor_copy(lo_wide[b][:], lo_cols[:, b:b + 1].to_broadcast([P, PASS]))
+
+        u_codes = [[sb("u_codes%d%d" % (b, a), [P, P], U32) for a in range(PASSES)] for b in range(BLOCKS)]
+        u_scales = [[sb("u_scales%d%d" % (b, a), [P, P], U8) for a in range(PASSES)] for b in range(BLOCKS)]
+        g_codes = [sb("g_codes%d" % a, [P, N], U32) for a in range(PASSES)]
+        g_scales = [sb("g_scales%d" % a, [P, N], U8) for a in range(PASSES)]
+
+        def entries(lst, a):
+            return lst[:, a * LIST_COLS:(a + 1) * LIST_COLS]
+
+        def slots(row, a):
+            return row[:, a * PASS:(a + 1) * PASS]
+
+        def turn_over(name, rounded):
+            words = rounded[:].bitcast(F32)
+            bank = turn.tile([P, 2, P], F32, name="turn_bank", tag="turn")
+            for h in range(2):
+                nc.tensor.transpose(bank[:, h, :], words[:, h:PASS // 2:2], ident[:])
+            grouped = sb(name, [P, PASS], BF16)
+            nc.scalar.copy(grouped[:].bitcast(F32).rearrange("p (r h) -> p r h", h=2),
+                           bank[:].rearrange("p h r -> p r h"))
+            return grouped
+
+        def gather_g(b, a):
+            picked = sb("g_picked%d%d" % (b, a), [P, PASS])
+            nc.vector.tensor_tensor(picked[:], g_tab[b][:].indirect(entries(list_g, a)), slots(rb_row, a), ALU.mult)
+            return picked
+
+        def gather_s(b, a, on_vector):
+            picked = sb("s_picked%d%d" % (b, a), [P, PASS])
+            window = s_tab[b][:].indirect(entries(list_g, a))
+            if on_vector:
+                nc.vector.tensor_copy(picked[:], window)
+            else:
+                nc.scalar.activation(picked[:], window, ACT.Copy)
+            return picked
+
+        def round_g(b, a, g_picked, s_picked):
+            rounded = sb("g_rounded%d%d" % (b, a), [P, PASS], BF16)
+            nc.vector.scalar_tensor_tensor(rounded[:], s_picked[:], 0.0, g_picked[:], ALU.max, ALU.mult)
+            return turn_over("g_grouped%d%d" % (b, a), rounded)
+
+        def quantise_g(b, a, grouped):
+            cols = slice(b * P, (b + 1) * P)
+            nc.vector.quantize_mx(g_codes[a][:, cols].bitcast(E5M2), g_scales[a][:, cols], grouped[:])
+
+        def quantise_u(b, a, grouped):
+            nc.vector.quantize_mx(u_codes[b][a][:].bitcast(E4M3), u_scales[b][a][:], grouped[:])
+
+        def gather_x(b):
+            over = sb("x_over%d" % b, [P, PASS])
+            nc.vector.tensor_tensor(over[:], x_tab[b][:].indirect(entries(list_x, 0)), lo_wide[b][:], ALU.subtract)
+            picked = sb("x_picked%d" % b, [P, PASS])
+            nc.scalar.activation(picked[:], x_tab[b][:].indirect(entries(list_x, 1)), ACT.Copy)
+            excess = sb("x_excess%d" % b, [P, PASS])
+            nc.scalar.activation(excess[:], picked[:], ACT.Relu, bias=neg_lo[:, b:b + 1])
+            return over, excess
+
+        def round_x0(b, over):
+            rounded = sb("u_rounded%d0" % b, [P, PASS], BF16)
+            nc.vector.scalar_tensor_tensor(rounded[:], over[:], 0.0, slots(ra_row, 0), ALU.max, ALU.mult)
+            return turn_over("u_grouped%d0" % b, rounded)
+
+        def round_x1(b, excess):
+            rounded = sb("u_rounded%d1" % b, [P, PASS], BF16)
+            nc.vector.tensor_tensor(rounded[:], excess[:], slots(ra_row, 1), ALU.mult)
+            return turn_over("u_grouped%d1" % b, rounded)
+
+        def multiply(b, acc, a):
+            nc.tensor.matmul_mx(acc[:], lhsT=u_codes[b][a][:].bitcast(E4M3), lhsT_scale=u_scales[b][a][:],
+                                rhs=g_codes[a][:].bitcast(E5M2), rhs_scale=g_scales[a][:],
+                                start=(a == 0), stop=(a == PASSES - 1))
+
+        def finish(b, acc):
+            wb = sb("wb%d" % b, [P, N])
+            total = sb("total%d" % b, [P, 1])
+            nc.vector.scalar_tensor_tensor(wb[:], acc[:], 1.0, bn_row[:], ALU.mult, ALU.add, accum_out=total[:])
+            size = sb("size%d" % b, [P, N])
+            size_sum = sb("size_sum%d" % b, [P, 1])
+            nc.scalar.activation(size[:], wb[:], ACT.Abs, bias=total[:], scale=-float(N), accum_out=size_sum[:])
+            centred = sb("centred%d" % b, [P, N])
+            nc.vector.tensor_scalar(centred[:], wb[:], float(N), total[:], ALU.mult, ALU.subtract)
+            denom = sb("denom%d" % b, [P, 1])
+            nc.vector.tensor_scalar(denom[:], size_sum[:], 1.0 / (N * N), 2.0, ALU.mult, ALU.add)
+            inverse = sb("inverse%d" % b, [P, 1])
+            nc.vector.reciprocal(inverse[:], denom[:])
+            result = sb("result%d" % b, [P, N])
+            nc.vector.tensor_scalar(result[:], centred[:], inverse[:], gk_scaled[:, b:b + 1], ALU.mult, ALU.mult)
+            nc.sync.dma_start(out_rows[b], result[:])
+
+        acc = [sums.tile([P, N], F32, name="acc%d" % b) for b in range(BLOCKS)]
+
+        g_picked = [gather_g(0, a) for a in range(PASSES)]
+        s_picked = [gather_s(0, a, a == 1) for a in range(PASSES)]
+        g_grouped = [round_g(0, a, g_picked[a], s_picked[a]) for a in range(PASSES)]
+        over, excess = gather_x(0)
+        quantise_g(0, 0, g_grouped[0])
+        u_grouped0 = round_x0(0, over)
+        quantise_g(0, 1, g_grouped[1])
+        u_grouped1 = round_x1(0, excess)
+        g_picked = [gather_g(1, a) for a in range(PASSES)]
+        quantise_u(0, 0, u_grouped0)
+        quantise_u(0, 1, u_grouped1)
+        s_picked = [gather_s(1, a, False) for a in range(PASSES)]
+        g_grouped0 = round_g(1, 0, g_picked[0], s_picked[0])
+        over, excess = gather_x(1)
+        g_grouped1 = round_g(1, 1, g_picked[1], s_picked[1])
+        u_grouped0 = round_x0(1, over)
+        u_grouped1 = round_x1(1, excess)
+        quantise_g(1, 0, g_grouped0)
+        quantise_g(1, 1, g_grouped1)
+        multiply(0, acc[0], 0)
+        multiply(0, acc[0], 1)
+        quantise_u(1, 0, u_grouped0)
+        multiply(1, acc[1], 0)
+        quantise_u(1, 1, u_grouped1)
+        multiply(1, acc[1], 1)
+        finish(0, acc[0])
+        finish(1, acc[1])

@@ -27,19 +27,24 @@ def tile_list_moment_over_saved_spread_kernel(tc, xf, ra, lo, gt, rb, sv, gk, bn
     nc = tc.nc
     with ExitStack() as ctx:
         keep = ctx.enter_context(tc.tile_pool(name="keep", bufs=1))
+        shared = ctx.enter_context(tc.tile_pool(name="shared", bufs=1))
         turn = ctx.enter_context(tc.psum_pool(name="turn", bufs=6))
         sums = ctx.enter_context(tc.psum_pool(name="sums", bufs=1))
 
-        def sb(name, shape, dtype=F32):
-            return keep.tile(shape, dtype, name=name, align_bytes=64)
+        def sb(name, shape, dtype=F32, tag=None):
+            return keep.tile(shape, dtype, name=name, tag=tag or name, align_bytes=64)
+
+        def at(offset, name, shape, dtype=F32):
+            return shared.tile(shape, dtype, name=name, offset=offset, align_bytes=64)
 
         list_x = keep.tile([P, J // 16], U16, name="list_x")
         list_g = keep.tile([P, J // 16], U16, name="list_g")
-        x_tab = [sb("x_tab%d" % b, [P, T]) for b in range(BLOCKS)]
+        x_tab = [at(PASS * 4 + 2 * T * 4, "x_tab0", [P, T]), sb("x_tab1", [P, T])]
         g_tab = [sb("g_tab%d" % b, [P, T]) for b in range(BLOCKS)]
-        s_tab = [sb("s_tab%d" % b, [P, T]) for b in range(BLOCKS)]
-        rb_cols = sb("rb_cols", [P, J // P])
-        ra_cols = sb("ra_cols", [P, J // P])
+        F = PASS * 4
+        s_tab = [at(F + b * T * 4, "s_tab%d" % b, [P, T]) for b in range(BLOCKS)]
+        rb_cols = sb("rb_cols", [P, PASSES, 8])
+        ra_cols = sb("ra_cols", [P, PASSES, 8], tag="left")
         bn_cols = sb("bn_cols", [P, N // P])
         lo_cols = sb("lo_cols", [P, BLOCKS])
         gk_cols = sb("gk_cols", [P, BLOCKS])
@@ -47,15 +52,15 @@ def tile_list_moment_over_saved_spread_kernel(tc, xf, ra, lo, gt, rb, sv, gk, bn
         x_rows = xf.rearrange("(p b) t -> b p t", b=BLOCKS)
         out_rows = out.rearrange("(p b) n -> b p n", b=BLOCKS)
 
-        nc.sync.dma_start(rb_cols[:], rb.rearrange("o (p c) -> (o p) c", p=P))
-        nc.sync.dma_start(list_g[:], offs2)
-        nc.sync.dma_start(g_tab[0][:], gt[0:P, :])
-        nc.sync.dma_start(ra_cols[:], ra.rearrange("o (p c) -> (o p) c", p=P))
-        nc.sync.dma_start(lo_cols[:], lo.rearrange("(p b) o -> p (b o)", b=BLOCKS))
-        nc.sync.dma_start(s_tab[0][:], sv[0:P, :])
-        nc.sync.dma_start(list_x[:], offs)
+        nc.sync.dma_start(ra_cols[:, :, 0:4], ra.rearrange("o (a p c) -> p (o a) c", a=PASSES, p=P))
+        nc.scalar.dma_start(lo_cols[:], lo.rearrange("(p b) o -> p (b o)", b=BLOCKS))
         nc.sync.dma_start(x_tab[0][:], x_rows[0])
+        nc.sync.dma_start(list_x[:], offs)
+        nc.sync.dma_start(list_g[:], offs2)
+        nc.scalar.dma_start(rb_cols[:, :, 0:4], rb.rearrange("o (a p c) -> p (o a) c", a=PASSES, p=P))
+        nc.sync.dma_start(g_tab[0][:], gt[0:P, :])
         nc.sync.dma_start(bn_cols[:], bn.rearrange("o (p c) -> (o p) c", p=P))
+        nc.sync.dma_start(s_tab[0][:], sv[0:P, :])
         nc.sync.dma_start(gk_cols[:], gk.rearrange("(p b) o -> p (b o)", b=BLOCKS))
         nc.sync.dma_start(g_tab[1][:], gt[P:2 * P, :])
         nc.sync.dma_start(s_tab[1][:], sv[P:2 * P, :])
@@ -64,32 +69,26 @@ def tile_list_moment_over_saved_spread_kernel(tc, xf, ra, lo, gt, rb, sv, gk, bn
         ident = sb("ident", [P, P])
         make_identity(nc, ident[:])
 
-        def spread(name, cols, count):
-            row = sb(name, [P, P * count])
-            row_v = row[:].rearrange("m (p c) -> m p c", c=count)
-            for c0 in range(0, count, 4):
-                width = min(4, count - c0)
-                bank = turn.tile([P, width, P], F32, name="turn_bank", tag="turn")
-                for c in range(width):
-                    nc.tensor.transpose(bank[:, c, :], cols[:, c0 + c:c0 + c + 1].to_broadcast([P, P]), ident[:])
-                nc.scalar.copy(row_v[:, :, c0:c0 + width], bank[:].rearrange("m c p -> m p c"))
+        def spread(row, cols, count, copy):
+            bank = turn.tile([P, count, P], F32, name="turn_bank", tag="turn")
+            for c in range(count):
+                nc.tensor.transpose(bank[:, c, :], cols[:, c:c + 1].to_broadcast([P, P]), ident[:])
+            copy(row[:].rearrange("m (p c) -> m p c", c=count), bank[:].rearrange("m c p -> m p c"))
             return row
 
-        rb_row = spread("rb_row", rb_cols, J // P)
-        ra_row = spread("ra_row", ra_cols, J // P)
-        bn_row = spread("bn_row", bn_cols, N // P)
-
         neg_lo = sb("neg_lo", [P, BLOCKS])
-        nc.vector.tensor_scalar(neg_lo[:], lo_cols[:], -1.0, None, ALU.mult)
-        gk_scaled = sb("gk_scaled", [P, BLOCKS])
-        nc.vector.tensor_scalar(gk_scaled[:], gk_cols[:], 1.0 / N, None, ALU.mult)
-        lo_wide = [sb("lo_wide%d" % b, [P, PASS]) for b in range(BLOCKS)]
+        nc.scalar.activation(neg_lo[:], lo_cols[:], ACT.Copy, scale=-1.0)
+        lo_wide = [sb("lo_wide0", [P, PASS]), at(0, "lo_wide1", [P, PASS])]
         for b in range(BLOCKS):
-            nc.vector.tensor_copy(lo_wide[b][:], lo_cols[:, b:b + 1].to_broadcast([P, PASS]))
+            nc.scalar.copy(lo_wide[b][:], lo_cols[:, b:b + 1].to_broadcast([P, PASS]))
+        ra_row = [spread(sb("ra_row%d" % a, [P, PASS]), ra_cols[:, a, :], 4, nc.vector.tensor_copy) for a in range(PASSES)]
+        rb_row = [at(F + 2 * T * 4 + a * F, "rb_row%d" % a, [P, PASS]) for a in range(PASSES)]
+        bn_row = at(3 * F + 2 * T * 4, "bn_row", [P, N])
 
-        u_codes = [[sb("u_codes%d%d" % (b, a), [P, P], U32) for a in range(PASSES)] for b in range(BLOCKS)]
         u_scales = [[sb("u_scales%d%d" % (b, a), [P, P], U8) for a in range(PASSES)] for b in range(BLOCKS)]
-        g_codes = [sb("g_codes%d" % a, [P, N], U32) for a in range(PASSES)]
+        u_codes = [[at(F + a * P * 4, "u_codes0%d" % a, [P, P], U32) for a in range(PASSES)],
+                   [sb("u_codes1%d" % a, [P, P], U32) for a in range(PASSES)]]
+        g_codes = [at(F + T * 4 + a * N * 4, "g_codes%d" % a, [P, N], U32) for a in range(PASSES)]
         g_scales = [sb("g_scales%d" % a, [P, N], U8) for a in range(PASSES)]
 
         def entries(lst, a):
@@ -98,34 +97,31 @@ def tile_list_moment_over_saved_spread_kernel(tc, xf, ra, lo, gt, rb, sv, gk, bn
         def slots(row, a):
             return row[:, a * PASS:(a + 1) * PASS]
 
-        def turn_over(name, rounded):
+        def turn_over(rounded):
             words = rounded[:].bitcast(F32)
             bank = turn.tile([P, 2, P], F32, name="turn_bank", tag="turn")
             for h in range(2):
                 nc.tensor.transpose(bank[:, h, :], words[:, h:PASS // 2:2], ident[:])
-            grouped = sb(name, [P, PASS], BF16)
+            return bank
+
+        def interleave(bank, grouped):
             nc.scalar.copy(grouped[:].bitcast(F32).rearrange("p (r h) -> p r h", h=2),
                            bank[:].rearrange("p h r -> p r h"))
             return grouped
 
-        def gather_g(b, a):
-            picked = sb("g_picked%d%d" % (b, a), [P, PASS])
-            nc.vector.tensor_tensor(picked[:], g_tab[b][:].indirect(entries(list_g, a)), slots(rb_row, a), ALU.mult)
-            return picked
+        def gather_g(b, a, picked):
+            nc.vector.tensor_tensor(picked[:], g_tab[b][:].indirect(entries(list_g, a)), rb_row[a][:], ALU.mult)
 
-        def gather_s(b, a, on_vector):
-            picked = sb("s_picked%d%d" % (b, a), [P, PASS])
-            window = s_tab[b][:].indirect(entries(list_g, a))
-            if on_vector:
-                nc.vector.tensor_copy(picked[:], window)
-            else:
-                nc.scalar.activation(picked[:], window, ACT.Copy)
-            return picked
+        def gather_s(b, picked):
+            half = PASS // 2
+            last = entries(list_g, 1)
+            nc.scalar.activation(picked[0][:], s_tab[b][:].indirect(entries(list_g, 0)), ACT.Copy)
+            nc.vector.tensor_copy(picked[1][:, half:], s_tab[b][:].indirect(last[:, LIST_COLS // 2:]))
+            nc.scalar.activation(picked[1][:, :half], s_tab[b][:].indirect(last[:, :LIST_COLS // 2]), ACT.Copy)
 
-        def round_g(b, a, g_picked, s_picked):
-            rounded = sb("g_rounded%d%d" % (b, a), [P, PASS], BF16)
+        def round_g(b, a, g_picked, s_picked, rounded):
             nc.vector.scalar_tensor_tensor(rounded[:], s_picked[:], 0.0, g_picked[:], ALU.max, ALU.mult)
-            return turn_over("g_grouped%d%d" % (b, a), rounded)
+            return turn_over(rounded)
 
         def quantise_g(b, a, grouped):
             cols = slice(b * P, (b + 1) * P)
@@ -134,24 +130,18 @@ def tile_list_moment_over_saved_spread_kernel(tc, xf, ra, lo, gt, rb, sv, gk, bn
         def quantise_u(b, a, grouped):
             nc.vector.quantize_mx(u_codes[b][a][:].bitcast(E4M3), u_scales[b][a][:], grouped[:])
 
-        def gather_x(b):
-            over = sb("x_over%d" % b, [P, PASS])
+        def gather_x(b, over, picked, excess):
             nc.vector.tensor_tensor(over[:], x_tab[b][:].indirect(entries(list_x, 0)), lo_wide[b][:], ALU.subtract)
-            picked = sb("x_picked%d" % b, [P, PASS])
             nc.scalar.activation(picked[:], x_tab[b][:].indirect(entries(list_x, 1)), ACT.Copy)
-            excess = sb("x_excess%d" % b, [P, PASS])
             nc.scalar.activation(excess[:], picked[:], ACT.Relu, bias=neg_lo[:, b:b + 1])
-            return over, excess
 
-        def round_x0(b, over):
-            rounded = sb("u_rounded%d0" % b, [P, PASS], BF16)
-            nc.vector.scalar_tensor_tensor(rounded[:], over[:], 0.0, slots(ra_row, 0), ALU.max, ALU.mult)
-            return turn_over("u_grouped%d0" % b, rounded)
+        def round_x0(b, over, rounded):
+            nc.vector.scalar_tensor_tensor(rounded[:], over[:], 0.0, ra_row[0][:], ALU.max, ALU.mult)
+            return interleave(turn_over(rounded), sb("u_grouped%d0" % b, [P, PASS], BF16))
 
-        def round_x1(b, excess):
-            rounded = sb("u_rounded%d1" % b, [P, PASS], BF16)
-            nc.vector.tensor_tensor(rounded[:], excess[:], slots(ra_row, 1), ALU.mult)
-            return turn_over("u_grouped%d1" % b, rounded)
+        def round_x1(b, excess, rounded):
+            nc.vector.tensor_tensor(rounded[:], excess[:], ra_row[1][:], ALU.mult)
+            return interleave(turn_over(rounded), sb("u_grouped%d1" % b, [P, PASS], BF16))
 
         def multiply(b, acc, a):
             nc.tensor.matmul_mx(acc[:], lhsT=u_codes[b][a][:].bitcast(E4M3), lhsT_scale=u_scales[b][a][:],
@@ -168,32 +158,50 @@ def tile_list_moment_over_saved_spread_kernel(tc, xf, ra, lo, gt, rb, sv, gk, bn
             centred = sb("centred%d" % b, [P, N])
             nc.vector.tensor_scalar(centred[:], wb[:], float(N), total[:], ALU.mult, ALU.subtract)
             denom = sb("denom%d" % b, [P, 1])
-            nc.vector.tensor_scalar(denom[:], size_sum[:], 1.0 / (N * N), 2.0, ALU.mult, ALU.add)
+            nc.vector.tensor_scalar(denom[:], size_sum[:], 1.0 / N, 2.0 * N, ALU.mult, ALU.add)
             inverse = sb("inverse%d" % b, [P, 1])
             nc.vector.reciprocal(inverse[:], denom[:])
             result = sb("result%d" % b, [P, N])
-            nc.vector.tensor_scalar(result[:], centred[:], inverse[:], gk_scaled[:, b:b + 1], ALU.mult, ALU.mult)
+            nc.vector.tensor_scalar(result[:], centred[:], inverse[:], gk_cols[:, b:b + 1], ALU.mult, ALU.mult)
             nc.sync.dma_start(out_rows[b], result[:])
 
         acc = [sums.tile([P, N], F32, name="acc%d" % b) for b in range(BLOCKS)]
 
-        g_picked = [gather_g(0, a) for a in range(PASSES)]
-        s_picked = [gather_s(0, a, a == 1) for a in range(PASSES)]
-        g_grouped = [round_g(0, a, g_picked[a], s_picked[a]) for a in range(PASSES)]
-        over, excess = gather_x(0)
-        quantise_g(0, 0, g_grouped[0])
-        u_grouped0 = round_x0(0, over)
-        quantise_g(0, 1, g_grouped[1])
-        u_grouped1 = round_x1(0, excess)
-        g_picked = [gather_g(1, a) for a in range(PASSES)]
+        over = sb("x_over0", [P, PASS], tag="left")
+        excess = sb("x_excess0", [P, PASS])
+        gather_x(0, over, sb("x_picked0", [P, PASS]), excess)
+        for a in range(PASSES):
+            spread(rb_row[a], rb_cols[:, a, :], 4, nc.scalar.copy)
+        u_grouped0 = round_x0(0, over, sb("u_rounded00", [P, PASS], BF16))
+        u_grouped1 = round_x1(0, excess, sb("u_rounded01", [P, PASS], BF16))
+        spread(bn_row, bn_cols[:], N // P, nc.scalar.copy)
+        g_picked = [sb("g_picked0%d" % a, [P, PASS]) for a in range(PASSES)]
+        gather_g(0, 0, g_picked[0])
         quantise_u(0, 0, u_grouped0)
+        gather_g(0, 1, g_picked[1])
         quantise_u(0, 1, u_grouped1)
-        s_picked = [gather_s(1, a, False) for a in range(PASSES)]
-        g_grouped0 = round_g(1, 0, g_picked[0], s_picked[0])
-        over, excess = gather_x(1)
-        g_grouped1 = round_g(1, 1, g_picked[1], s_picked[1])
-        u_grouped0 = round_x0(1, over)
-        u_grouped1 = round_x1(1, excess)
+        s_picked = [sb("s_picked0%d" % a, [P, PASS]) for a in range(PASSES)]
+        gather_s(0, s_picked)
+        g_grouped0 = interleave(round_g(0, 0, g_picked[0], s_picked[0], sb("g_rounded00", [P, PASS], BF16)),
+                                sb("g_grouped00", [P, PASS], BF16))
+        g_grouped1 = interleave(round_g(0, 1, g_picked[1], s_picked[1], sb("g_rounded01", [P, PASS], BF16)),
+                                sb("g_grouped01", [P, PASS], BF16))
+        g_picked = [sb("g_picked1%d" % a, [P, PASS]) for a in range(PASSES)]
+        quantise_g(0, 0, g_grouped0)
+        gather_g(1, 0, g_picked[0])
+        quantise_g(0, 1, g_grouped1)
+        gather_g(1, 1, g_picked[1])
+        s_picked = [sb("s_picked1%d" % a, [P, PASS]) for a in range(PASSES)]
+        gather_s(1, s_picked)
+        g_bank0 = round_g(1, 0, g_picked[0], s_picked[0], sb("g_rounded10", [P, PASS], BF16))
+        over = sb("x_over1", [P, PASS])
+        excess = sb("x_excess1", [P, PASS])
+        gather_x(1, over, sb("x_picked1", [P, PASS]), excess)
+        g_grouped0 = interleave(g_bank0, at(0, "g_grouped10", [P, PASS], BF16))
+        g_grouped1 = interleave(round_g(1, 1, g_picked[1], s_picked[1], at(F // 2, "g_rounded11", [P, PASS], BF16)),
+                                sb("g_grouped11", [P, PASS], BF16))
+        u_grouped0 = round_x0(1, over, sb("u_rounded10", [P, PASS], BF16))
+        u_grouped1 = round_x1(1, excess, sb("u_rounded11", [P, PASS], BF16))
         quantise_g(1, 0, g_grouped0)
         quantise_g(1, 1, g_grouped1)
         multiply(0, acc[0], 0)

@@ -39,13 +39,16 @@ def tile_list_moment_over_saved_spread_kernel(tc, xf, ra, lo, gt, rb, sv, gk, bn
 
         list_x = keep.tile([P, J // 16], U16, name="list_x")
         list_g = keep.tile([P, J // 16], U16, name="list_g")
-        x_tab = [at(PASS * 4 + 2 * T * 4, "x_tab0", [P, T]), sb("x_tab1", [P, T])]
-        g_tab = [sb("g_tab%d" % b, [P, T]) for b in range(BLOCKS)]
-        F = PASS * 4
-        s_tab = [at(F + b * T * 4, "s_tab%d" % b, [P, T]) for b in range(BLOCKS)]
+        W = PASS * 4
+        TAB = T * 4
+        A, B, C, D = 0, W, 2 * W, 5 * W + 64
+        X0, G0, G1, S1 = 6 * W, 6 * W + TAB, 6 * W + 2 * TAB, 6 * W + 3 * TAB
+        x_tab = [at(X0, "x_tab0", [P, T]), sb("x_tab1", [P, T])]
+        g_tab = [at(G0, "g_tab0", [P, T]), at(G1, "g_tab1", [P, T])]
+        s_tab = [sb("s_tab0", [P, T]), at(S1, "s_tab1", [P, T])]
         rb_cols = sb("rb_cols", [P, PASSES, 8])
-        ra_cols = sb("ra_cols", [P, PASSES, 8], tag="left")
-        bn_cols = sb("bn_cols", [P, N // P])
+        ra_cols = at(A, "ra_cols", [P, PASSES, 8])
+        bn_row = sb("bn_row", [P, N])
         lo_cols = sb("lo_cols", [P, BLOCKS])
         gk_cols = sb("gk_cols", [P, BLOCKS])
 
@@ -54,17 +57,17 @@ def tile_list_moment_over_saved_spread_kernel(tc, xf, ra, lo, gt, rb, sv, gk, bn
 
         nc.sync.dma_start(ra_cols[:, :, 0:4], ra.rearrange("o (a p c) -> p (o a) c", a=PASSES, p=P))
         nc.scalar.dma_start(lo_cols[:], lo.rearrange("(p b) o -> p (b o)", b=BLOCKS))
-        nc.sync.dma_start(x_tab[0][:], x_rows[0])
         nc.sync.dma_start(list_x[:], offs)
+        nc.sync.dma_start(x_tab[0][:], x_rows[0])
+        nc.sync.dma_start(rb_cols[:, :, 0:4], rb.rearrange("o (a p c) -> p (o a) c", a=PASSES, p=P))
         nc.sync.dma_start(list_g[:], offs2)
-        nc.scalar.dma_start(rb_cols[:, :, 0:4], rb.rearrange("o (a p c) -> p (o a) c", a=PASSES, p=P))
         nc.sync.dma_start(g_tab[0][:], gt[0:P, :])
-        nc.sync.dma_start(bn_cols[:], bn.rearrange("o (p c) -> (o p) c", p=P))
         nc.sync.dma_start(s_tab[0][:], sv[0:P, :])
-        nc.sync.dma_start(gk_cols[:], gk.rearrange("(p b) o -> p (b o)", b=BLOCKS))
         nc.sync.dma_start(g_tab[1][:], gt[P:2 * P, :])
         nc.sync.dma_start(s_tab[1][:], sv[P:2 * P, :])
         nc.sync.dma_start(x_tab[1][:], x_rows[1])
+        nc.sync.dma_start(bn_row[:], bn.rearrange("o n -> (o n)").partition_broadcast(P))
+        nc.sync.dma_start(gk_cols[:], gk.rearrange("(p b) o -> p (b o)", b=BLOCKS))
 
         ident = sb("ident", [P, P])
         make_identity(nc, ident[:])
@@ -78,24 +81,20 @@ def tile_list_moment_over_saved_spread_kernel(tc, xf, ra, lo, gt, rb, sv, gk, bn
 
         neg_lo = sb("neg_lo", [P, BLOCKS])
         nc.scalar.activation(neg_lo[:], lo_cols[:], ACT.Copy, scale=-1.0)
-        lo_wide = [sb("lo_wide0", [P, PASS]), at(0, "lo_wide1", [P, PASS])]
+        lo_wide = [sb("lo_wide%d" % b, [P, PASS]) for b in range(BLOCKS)]
         for b in range(BLOCKS):
             nc.scalar.copy(lo_wide[b][:], lo_cols[:, b:b + 1].to_broadcast([P, PASS]))
         ra_row = [spread(sb("ra_row%d" % a, [P, PASS]), ra_cols[:, a, :], 4, nc.vector.tensor_copy) for a in range(PASSES)]
-        rb_row = [at(F + 2 * T * 4 + a * F, "rb_row%d" % a, [P, PASS]) for a in range(PASSES)]
-        bn_row = at(3 * F + 2 * T * 4, "bn_row", [P, N])
+        rb_row = [at(X0 + a * W, "rb_row%d" % a, [P, PASS]) for a in range(PASSES)]
 
-        u_scales = [[sb("u_scales%d%d" % (b, a), [P, P], U8) for a in range(PASSES)] for b in range(BLOCKS)]
-        u_codes = [[at(F + a * P * 4, "u_codes0%d" % a, [P, P], U32) for a in range(PASSES)],
+        u_codes = [[at(G0 + a * P * 4, "u_codes0%d" % a, [P, P], U32) for a in range(PASSES)],
                    [sb("u_codes1%d" % a, [P, P], U32) for a in range(PASSES)]]
-        g_codes = [at(F + T * 4 + a * N * 4, "g_codes%d" % a, [P, N], U32) for a in range(PASSES)]
+        u_scales = [[sb("u_scales%d%d" % (b, a), [P, P], U8) for a in range(PASSES)] for b in range(BLOCKS)]
+        g_codes = [at(X0 + W, "g_codes0", [P, N], U32), sb("g_codes1", [P, N], U32)]
         g_scales = [sb("g_scales%d" % a, [P, N], U8) for a in range(PASSES)]
 
         def entries(lst, a):
             return lst[:, a * LIST_COLS:(a + 1) * LIST_COLS]
-
-        def slots(row, a):
-            return row[:, a * PASS:(a + 1) * PASS]
 
         def turn_over(rounded):
             words = rounded[:].bitcast(F32)
@@ -112,15 +111,11 @@ def tile_list_moment_over_saved_spread_kernel(tc, xf, ra, lo, gt, rb, sv, gk, bn
         def gather_g(b, a, picked):
             nc.vector.tensor_tensor(picked[:], g_tab[b][:].indirect(entries(list_g, a)), rb_row[a][:], ALU.mult)
 
-        def gather_s(b, picked):
-            half = PASS // 2
-            last = entries(list_g, 1)
-            nc.scalar.activation(picked[0][:], s_tab[b][:].indirect(entries(list_g, 0)), ACT.Copy)
-            nc.vector.tensor_copy(picked[1][:, half:], s_tab[b][:].indirect(last[:, LIST_COLS // 2:]))
-            nc.scalar.activation(picked[1][:, :half], s_tab[b][:].indirect(last[:, :LIST_COLS // 2]), ACT.Copy)
+        def gather_s(b, picked, columns):
+            nc.scalar.activation(picked, s_tab[b][:].indirect(columns), ACT.Copy)
 
         def round_g(b, a, g_picked, s_picked, rounded):
-            nc.vector.scalar_tensor_tensor(rounded[:], s_picked[:], 0.0, g_picked[:], ALU.max, ALU.mult)
+            nc.vector.scalar_tensor_tensor(rounded[:], s_picked, 0.0, g_picked[:], ALU.max, ALU.mult)
             return turn_over(rounded)
 
         def quantise_g(b, a, grouped):
@@ -167,43 +162,45 @@ def tile_list_moment_over_saved_spread_kernel(tc, xf, ra, lo, gt, rb, sv, gk, bn
 
         acc = [sums.tile([P, N], F32, name="acc%d" % b) for b in range(BLOCKS)]
 
-        over = sb("x_over0", [P, PASS], tag="left")
+        over = at(A, "x_over0", [P, PASS])
         excess = sb("x_excess0", [P, PASS])
         gather_x(0, over, sb("x_picked0", [P, PASS]), excess)
         for a in range(PASSES):
             spread(rb_row[a], rb_cols[:, a, :], 4, nc.scalar.copy)
-        u_grouped0 = round_x0(0, over, sb("u_rounded00", [P, PASS], BF16))
-        u_grouped1 = round_x1(0, excess, sb("u_rounded01", [P, PASS], BF16))
-        spread(bn_row, bn_cols[:], N // P, nc.scalar.copy)
-        g_picked = [sb("g_picked0%d" % a, [P, PASS]) for a in range(PASSES)]
+        u_grouped0 = round_x0(0, over, at(B, "u_rounded00", [P, PASS], BF16))
+        u_grouped1 = round_x1(0, excess, at(A, "u_rounded01", [P, PASS], BF16))
+        g_picked = [at(C, "g_picked00", [P, PASS]), sb("g_picked01", [P, PASS])]
         gather_g(0, 0, g_picked[0])
-        quantise_u(0, 0, u_grouped0)
         gather_g(0, 1, g_picked[1])
-        quantise_u(0, 1, u_grouped1)
-        s_picked = [sb("s_picked0%d" % a, [P, PASS]) for a in range(PASSES)]
-        gather_s(0, s_picked)
-        g_grouped0 = interleave(round_g(0, 0, g_picked[0], s_picked[0], sb("g_rounded00", [P, PASS], BF16)),
+        s_picked = [at(B, "s_picked00", [P, PASS])[:], at(A, "s_picked01", [P, PASS])[:]]
+        for a in range(PASSES):
+            gather_s(0, s_picked[a], entries(list_g, a))
+        g_grouped0 = interleave(round_g(0, 0, g_picked[0], s_picked[0], at(C + W, "g_rounded00", [P, PASS], BF16)),
                                 sb("g_grouped00", [P, PASS], BF16))
-        g_grouped1 = interleave(round_g(0, 1, g_picked[1], s_picked[1], sb("g_rounded01", [P, PASS], BF16)),
-                                sb("g_grouped01", [P, PASS], BF16))
-        g_picked = [sb("g_picked1%d" % a, [P, PASS]) for a in range(PASSES)]
+        quantise_u(0, 0, u_grouped0)
+        quantise_u(0, 1, u_grouped1)
+        g_next = [at(C, "g_picked10", [P, PASS]), at(C + W, "g_picked11", [P, PASS])]
+        gather_g(1, 0, g_next[0])
+        gather_g(1, 1, g_next[1])
+        g_bank = round_g(0, 1, g_picked[1], s_picked[1], at(X0 + 64, "g_rounded01", [P, PASS], BF16))
         quantise_g(0, 0, g_grouped0)
-        gather_g(1, 0, g_picked[0])
+        g_picked = g_next
+        s_picked = [at(D, "s_picked10", [P, PASS])[:], at(G1, "s_picked11", [P, PASS])[:]]
+        gather_s(1, s_picked[0], entries(list_g, 0))
+        last = entries(list_g, 1)
+        nc.vector.tensor_copy(s_picked[1][:, PASS // 2:], s_tab[1][:].indirect(last[:, LIST_COLS // 2:]))
+        gather_s(1, s_picked[1][:, :PASS // 2], last[:, :LIST_COLS // 2])
+        g_grouped1 = interleave(g_bank, at(S1, "g_grouped01", [P, PASS], BF16))
+        g_banks = [round_g(1, a, g_picked[a], s_picked[a], sb("g_rounded1%d" % a, [P, PASS], BF16)) for a in range(PASSES)]
         quantise_g(0, 1, g_grouped1)
-        gather_g(1, 1, g_picked[1])
-        s_picked = [sb("s_picked1%d" % a, [P, PASS]) for a in range(PASSES)]
-        gather_s(1, s_picked)
-        g_bank0 = round_g(1, 0, g_picked[0], s_picked[0], sb("g_rounded10", [P, PASS], BF16))
-        over = sb("x_over1", [P, PASS])
+        over = at(C, "x_over1", [P, PASS])
         excess = sb("x_excess1", [P, PASS])
-        gather_x(1, over, sb("x_picked1", [P, PASS]), excess)
-        g_grouped0 = interleave(g_bank0, at(0, "g_grouped10", [P, PASS], BF16))
-        g_grouped1 = interleave(round_g(1, 1, g_picked[1], s_picked[1], at(F // 2, "g_rounded11", [P, PASS], BF16)),
-                                sb("g_grouped11", [P, PASS], BF16))
+        gather_x(1, over, at(D, "x_picked1", [P, PASS]), excess)
+        g_grouped = [interleave(g_banks[a], at(D + a * W // 2, "g_grouped1%d" % a, [P, PASS], BF16)) for a in range(PASSES)]
         u_grouped0 = round_x0(1, over, sb("u_rounded10", [P, PASS], BF16))
         u_grouped1 = round_x1(1, excess, sb("u_rounded11", [P, PASS], BF16))
-        quantise_g(1, 0, g_grouped0)
-        quantise_g(1, 1, g_grouped1)
+        quantise_g(1, 0, g_grouped[0])
+        quantise_g(1, 1, g_grouped[1])
         multiply(0, acc[0], 0)
         multiply(0, acc[0], 1)
         quantise_u(1, 0, u_grouped0)

@@ -42,12 +42,12 @@ def tile_list_moment_over_saved_spread_kernel(tc, xf, ra, lo, gt, rb, sv, gk, bn
         W = PASS * 4
         TAB = T * 4
         A, B, C, D = 0, W, 2 * W, 5 * W + 64
-        X0, G0, G1, S1 = 6 * W, 6 * W + TAB, 6 * W + 2 * TAB, 6 * W + 3 * TAB
-        x_tab = [at(X0, "x_tab0", [P, T]), sb("x_tab1", [P, T])]
+        X0, G0, G1, S1, X1 = [6 * W + i * TAB for i in range(5)]
+        x_tab = [at(X0, "x_tab0", [P, T]), at(X1, "x_tab1", [P, T])]
         g_tab = [at(G0, "g_tab0", [P, T]), at(G1, "g_tab1", [P, T])]
         s_tab = [sb("s_tab0", [P, T]), at(S1, "s_tab1", [P, T])]
         rb_cols = sb("rb_cols", [P, PASSES, 8])
-        ra_cols = at(A, "ra_cols", [P, PASSES, 8])
+        ra_cols = sb("ra_cols", [P, PASSES, 8])
         bn_row = sb("bn_row", [P, N])
         lo_cols = sb("lo_cols", [P, BLOCKS])
         gk_cols = sb("gk_cols", [P, BLOCKS])
@@ -84,7 +84,7 @@ def tile_list_moment_over_saved_spread_kernel(tc, xf, ra, lo, gt, rb, sv, gk, bn
         lo_wide = [sb("lo_wide%d" % b, [P, PASS]) for b in range(BLOCKS)]
         for b in range(BLOCKS):
             nc.scalar.copy(lo_wide[b][:], lo_cols[:, b:b + 1].to_broadcast([P, PASS]))
-        ra_row = [spread(sb("ra_row%d" % a, [P, PASS]), ra_cols[:, a, :], 4, nc.vector.tensor_copy) for a in range(PASSES)]
+        ra_row = spread(sb("ra_row", [P, PASS]), ra_cols[:, 0, :], 4, nc.vector.tensor_copy)
         rb_row = [at(X0 + a * W, "rb_row%d" % a, [P, PASS]) for a in range(PASSES)]
 
         u_codes = [[at(G0 + a * P * 4, "u_codes0%d" % a, [P, P], U32) for a in range(PASSES)],
@@ -125,23 +125,35 @@ def tile_list_moment_over_saved_spread_kernel(tc, xf, ra, lo, gt, rb, sv, gk, bn
         def quantise_u(b, a, grouped):
             nc.vector.quantize_mx(u_codes[b][a][:].bitcast(E4M3), u_scales[b][a][:], grouped[:])
 
-        def gather_x(b, over, picked, excess):
+        def gather_x(b, over, picked):
             nc.vector.tensor_tensor(over[:], x_tab[b][:].indirect(entries(list_x, 0)), lo_wide[b][:], ALU.subtract)
             nc.scalar.activation(picked[:], x_tab[b][:].indirect(entries(list_x, 1)), ACT.Copy)
-            nc.scalar.activation(excess[:], picked[:], ACT.Relu, bias=neg_lo[:, b:b + 1])
 
         def round_x0(b, over, rounded):
-            nc.vector.scalar_tensor_tensor(rounded[:], over[:], 0.0, ra_row[0][:], ALU.max, ALU.mult)
+            nc.vector.scalar_tensor_tensor(rounded[:], over[:], 0.0, ra_row[:], ALU.max, ALU.mult)
             return interleave(turn_over(rounded), sb("u_grouped%d0" % b, [P, PASS], BF16))
 
-        def round_x1(b, excess, rounded):
-            nc.vector.tensor_tensor(rounded[:], excess[:], ra_row[1][:], ALU.mult)
-            return interleave(turn_over(rounded), sb("u_grouped%d1" % b, [P, PASS], BF16))
+        def turn_x1(b, picked):
+            bank = turn.tile([P, 4, P], F32, name="turn_bank", tag="turn")
+            for t in range(4):
+                nc.tensor.matmul(bank[:, t, :], neg_lo[:, b:b + 1].to_broadcast([P, P]), ident[:],
+                                 start=(t == 0), stop=False, is_transpose=True)
+            for t in range(4):
+                nc.tensor.matmul(bank[:, t, :], picked[:, t:PASS:4], ident[:],
+                                 start=False, stop=(t == 3), is_transpose=True)
+            return bank
+
+        def round_x1(b, bank):
+            grouped = sb("u_grouped%d1" % b, [P, PASS], BF16)
+            nc.vector.scalar_tensor_tensor(grouped[:].rearrange("p (k t) -> p k t", t=4),
+                                           bank[:].rearrange("p t k -> p k t"), 0.0,
+                                           ra_cols[:, 1:2, 0:4].to_broadcast([P, P, 4]), ALU.max, ALU.mult)
+            return grouped
 
         def multiply(b, acc, a):
             nc.tensor.matmul_mx(acc[:], lhsT=u_codes[b][a][:].bitcast(E4M3), lhsT_scale=u_scales[b][a][:],
                                 rhs=g_codes[a][:].bitcast(E5M2), rhs_scale=g_scales[a][:],
-                                start=(a == 0), stop=(a == PASSES - 1))
+                                start=(a == PASSES - 1), stop=(a == 0))
 
         def finish(b, acc):
             wb = sb("wb%d" % b, [P, N])
@@ -162,13 +174,14 @@ def tile_list_moment_over_saved_spread_kernel(tc, xf, ra, lo, gt, rb, sv, gk, bn
 
         acc = [sums.tile([P, N], F32, name="acc%d" % b) for b in range(BLOCKS)]
 
-        over = at(A, "x_over0", [P, PASS])
-        excess = sb("x_excess0", [P, PASS])
-        gather_x(0, over, sb("x_picked0", [P, PASS]), excess)
+        over = sb("x_over0", [P, PASS])
+        picked = at(B, "x_picked0", [P, PASS])
+        gather_x(0, over, picked)
         for a in range(PASSES):
             spread(rb_row[a], rb_cols[:, a, :], 4, nc.scalar.copy)
-        u_grouped0 = round_x0(0, over, at(B, "u_rounded00", [P, PASS], BF16))
-        u_grouped1 = round_x1(0, excess, at(A, "u_rounded01", [P, PASS], BF16))
+        x_bank = turn_x1(0, picked)
+        u_grouped0 = round_x0(0, over, at(A, "u_rounded00", [P, PASS], BF16))
+        u_grouped1 = round_x1(0, x_bank)
         g_picked = [at(C, "g_picked00", [P, PASS]), sb("g_picked01", [P, PASS])]
         gather_g(0, 0, g_picked[0])
         gather_g(0, 1, g_picked[1])
@@ -194,18 +207,18 @@ def tile_list_moment_over_saved_spread_kernel(tc, xf, ra, lo, gt, rb, sv, gk, bn
         g_banks = [round_g(1, a, g_picked[a], s_picked[a], sb("g_rounded1%d" % a, [P, PASS], BF16)) for a in range(PASSES)]
         quantise_g(0, 1, g_grouped1)
         over = at(C, "x_over1", [P, PASS])
-        excess = sb("x_excess1", [P, PASS])
-        gather_x(1, over, at(D, "x_picked1", [P, PASS]), excess)
-        g_grouped = [interleave(g_banks[a], at(D + a * W // 2, "g_grouped1%d" % a, [P, PASS], BF16)) for a in range(PASSES)]
+        picked = at(D, "x_picked1", [P, PASS])
+        gather_x(1, over, picked)
+        x_bank = turn_x1(1, picked)
+        g_grouped = [interleave(g_banks[a], at(X1 + a * W // 2, "g_grouped1%d" % a, [P, PASS], BF16)) for a in range(PASSES)]
         u_grouped0 = round_x0(1, over, sb("u_rounded10", [P, PASS], BF16))
-        u_grouped1 = round_x1(1, excess, sb("u_rounded11", [P, PASS], BF16))
-        quantise_g(1, 0, g_grouped[0])
+        u_grouped1 = round_x1(1, x_bank)
         quantise_g(1, 1, g_grouped[1])
-        multiply(0, acc[0], 0)
-        multiply(0, acc[0], 1)
-        quantise_u(1, 0, u_grouped0)
-        multiply(1, acc[1], 0)
+        quantise_g(1, 0, g_grouped[0])
         quantise_u(1, 1, u_grouped1)
-        multiply(1, acc[1], 1)
+        quantise_u(1, 0, u_grouped0)
+        for b in range(BLOCKS):
+            multiply(b, acc[b], 1)
+            multiply(b, acc[b], 0)
         finish(0, acc[0])
         finish(1, acc[1])

from contextlib import ExitStack

import concourse.mybir as mybir
from concourse.masks import make_identity

K, J, N, T = 256, 1024, 256, 2048
FLOPS = 2 * K * J * N

F32 = mybir.dt.float32
BF16 = mybir.dt.bfloat16
U32 = mybir.dt.uint32
U16 = mybir.dt.uint16
U8 = mybir.dt.uint8
E4M3 = mybir.dt.float8_e4m3fn_x4
E5M2 = mybir.dt.float8_e5m2_x4
ALU = mybir.AluOpType
ACT = mybir.ActivationFunctionType

P = 128
PASS = 512
PASSES = J // PASS
BLOCKS = K // P
LIST_COLS = PASS // 16


def tile_list_moment_over_saved_spread_kernel(tc, xf, ra, lo, gt, rb, sv, gk, bn, offs, offs2, out):
    nc = tc.nc
    with ExitStack() as ctx:
        keep = ctx.enter_context(tc.tile_pool(name="keep", bufs=1))
        shared = ctx.enter_context(tc.tile_pool(name="shared", bufs=1))
        turn = ctx.enter_context(tc.psum_pool(name="turn", bufs=6))
        sums = ctx.enter_context(tc.psum_pool(name="sums", bufs=1))

        def sb(name, shape, dtype=F32, tag=None):
            return keep.tile(shape, dtype, name=name, tag=tag or name, align_bytes=64)

        def at(offset, name, shape, dtype=F32):
            return shared.tile(shape, dtype, name=name, offset=offset, align_bytes=64)

        list_x = keep.tile([P, J // 16], U16, name="list_x")
        list_g = keep.tile([P, J // 16], U16, name="list_g")
        W = PASS * 4
        TAB = T * 4
        A, B, C, D = 0, W, 2 * W, 5 * W + 64
        X0, G0, G1, S1, X1 = [6 * W + i * TAB for i in range(5)]
        x_tab = [at(X0, "x_tab0", [P, T]), at(X1, "x_tab1", [P, T])]
        g_tab = [at(G0, "g_tab0", [P, T]), at(G1, "g_tab1", [P, T])]
        s_tab = [sb("s_tab0", [P, T]), at(S1, "s_tab1", [P, T])]
        rb_cols = sb("rb_cols", [P, PASSES, 8])
        ra_cols = sb("ra_cols", [P, PASSES, 8])
        bn_row = sb("bn_row", [P, N])
        lo_cols = sb("lo_cols", [P, BLOCKS])
        gk_cols = sb("gk_cols", [P, BLOCKS])

        x_rows = xf.rearrange("(p b) t -> b p t", b=BLOCKS)
        out_rows = out.rearrange("(p b) n -> b p n", b=BLOCKS)

        nc.sync.dma_start(ra_cols[:, :, 0:4], ra.rearrange("o (a p c) -> p (o a) c", a=PASSES, p=P))
        nc.scalar.dma_start(lo_cols[:], lo.rearrange("(p b) o -> p (b o)", b=BLOCKS))
        nc.sync.dma_start(list_x[:], offs)
        nc.sync.dma_start(x_tab[0][:], x_rows[0])
        nc.sync.dma_start(rb_cols[:, :, 0:4], rb.rearrange("o (a p c) -> p (o a) c", a=PASSES, p=P))
        nc.sync.dma_start(list_g[:], offs2)
        nc.sync.dma_start(g_tab[0][:], gt[0:P, :])
        nc.sync.dma_start(s_tab[0][:], sv[0:P, :])
        nc.sync.dma_start(g_tab[1][:], gt[P:2 * P, :])
        nc.sync.dma_start(s_tab[1][:], sv[P:2 * P, :])
        nc.sync.dma_start(x_tab[1][:], x_rows[1])
        nc.sync.dma_start(bn_row[:], bn.rearrange("o n -> (o n)").partition_broadcast(P))
        nc.sync.dma_start(gk_cols[:], gk.rearrange("(p b) o -> p (b o)", b=BLOCKS))

        ident = sb("ident", [P, P])
        make_identity(nc, ident[:])

        def spread(row, cols, count, copy):
            bank = turn.tile([P, count, P], F32, name="turn_bank", tag="turn")
            for c in range(count):
                nc.tensor.transpose(bank[:, c, :], cols[:, c:c + 1].to_broadcast([P, P]), ident[:])
            copy(row[:].rearrange("m (p c) -> m p c", c=count), bank[:].rearrange("m c p -> m p c"))
            return row

        neg_lo = sb("neg_lo", [P, BLOCKS])
        nc.scalar.activation(neg_lo[:], lo_cols[:], ACT.Copy, scale=-1.0)
        lo_wide = [sb("lo_wide%d" % b, [P, PASS]) for b in range(BLOCKS)]
        for b in range(BLOCKS):
            nc.scalar.copy(lo_wide[b][:], lo_cols[:, b:b + 1].to_broadcast([P, PASS]))
        ra_row = spread(sb("ra_row", [P, PASS]), ra_cols[:, 0, :], 4, nc.vector.tensor_copy)
        rb_row = [at(X0 + a * W, "rb_row%d" % a, [P, PASS]) for a in range(PASSES)]

        u_codes = [[at(G0 + a * P * 4, "u_codes0%d" % a, [P, P], U32) for a in range(PASSES)],
                   [sb("u_codes1%d" % a, [P, P], U32) for a in range(PASSES)]]
        u_scales = [[sb("u_scales%d%d" % (b, a), [P, P], U8) for a in range(PASSES)] for b in range(BLOCKS)]
        g_codes = [at(X0 + W, "g_codes0", [P, N], U32), sb("g_codes1", [P, N], U32)]
        g_scales = [sb("g_scales%d" % a, [P, N], U8) for a in range(PASSES)]

        def entries(lst, a):
            return lst[:, a * LIST_COLS:(a + 1) * LIST_COLS]

        def turn_over(rounded):
            words = rounded[:].bitcast(F32)
            bank = turn.tile([P, 2, P], F32, name="turn_bank", tag="turn")
            for h in range(2):
                nc.tensor.transpose(bank[:, h, :], words[:, h:PASS // 2:2], ident[:])
            return bank

        def interleave(bank, grouped):
            nc.scalar.copy(grouped[:].bitcast(F32).rearrange("p (r h) -> p r h", h=2),
                           bank[:].rearrange("p h r -> p r h"))
            return grouped

        def gather_g(b, a, picked):
            nc.vector.tensor_tensor(picked[:], g_tab[b][:].indirect(entries(list_g, a)), rb_row[a][:], ALU.mult)

        def gather_s(b, picked, columns):
            nc.scalar.activation(picked, s_tab[b][:].indirect(columns), ACT.Copy)

        def round_g(b, a, g_picked, s_picked, rounded):
            nc.vector.scalar_tensor_tensor(rounded[:], s_picked, 0.0, g_picked[:], ALU.max, ALU.mult)
            return turn_over(rounded)

        def quantise_g(b, a, grouped):
            cols = slice(b * P, (b + 1) * P)
            nc.vector.quantize_mx(g_codes[a][:, cols].bitcast(E5M2), g_scales[a][:, cols], grouped[:])

        def quantise_u(b, a, grouped):
            nc.vector.quantize_mx(u_codes[b][a][:].bitcast(E4M3), u_scales[b][a][:], grouped[:])

        def gather_x(b, over, picked):
            nc.vector.tensor_tensor(over[:], x_tab[b][:].indirect(entries(list_x, 0)), lo_wide[b][:], ALU.subtract)
            nc.scalar.activation(picked[:], x_tab[b][:].indirect(entries(list_x, 1)), ACT.Copy)

        def round_x0(b, over, rounded):
            nc.vector.scalar_tensor_tensor(rounded[:], over[:], 0.0, ra_row[:], ALU.max, ALU.mult)
            return interleave(turn_over(rounded), sb("u_grouped%d0" % b, [P, PASS], BF16))

        def turn_x1(b, picked):
            bank = turn.tile([P, 4, P], F32, name="turn_bank", tag="turn")
            for t in range(4):
                nc.tensor.matmul(bank[:, t, :], neg_lo[:, b:b + 1].to_broadcast([P, P]), ident[:],
                                 start=(t == 0), stop=False, is_transpose=True)
            for t in range(4):
                nc.tensor.matmul(bank[:, t, :], picked[:, t:PASS:4], ident[:],
                                 start=False, stop=(t == 3), is_transpose=True)
            return bank

        def round_x1(b, bank):
            grouped = sb("u_grouped%d1" % b, [P, PASS], BF16)
            nc.vector.scalar_tensor_tensor(grouped[:].rearrange("p (k t) -> p k t", t=4),
                                           bank[:].rearrange("p t k -> p k t"), 0.0,
                                           ra_cols[:, 1:2, 0:4].to_broadcast([P, P, 4]), ALU.max, ALU.mult)
            return grouped

        def multiply(b, acc, a):
            nc.tensor.matmul_mx(acc[:], lhsT=u_codes[b][a][:].bitcast(E4M3), lhsT_scale=u_scales[b][a][:],
                                rhs=g_codes[a][:].bitcast(E5M2), rhs_scale=g_scales[a][:],
                                start=(a == PASSES - 1), stop=(a == 0))

        def finish(b, acc):
            wb = sb("wb%d" % b, [P, N])
            total = sb("total%d" % b, [P, 1])
            nc.vector.scalar_tensor_tensor(wb[:], acc[:], 1.0, bn_row[:], ALU.mult, ALU.add, accum_out=total[:])
            size = sb("size%d" % b, [P, N])
            size_sum = sb("size_sum%d" % b, [P, 1])
            nc.scalar.activation(size[:], wb[:], ACT.Abs, bias=total[:], scale=-float(N), accum_out=size_sum[:])
            centred = sb("centred%d" % b, [P, N])
            nc.vector.tensor_scalar(centred[:], wb[:], float(N), total[:], ALU.mult, ALU.subtract)
            denom = sb("denom%d" % b, [P, 1])
            nc.vector.tensor_scalar(denom[:], size_sum[:], 1.0 / N, 2.0 * N, ALU.mult, ALU.add)
            inverse = sb("inverse%d" % b, [P, 1])
            nc.vector.reciprocal(inverse[:], denom[:])
            result = sb("result%d" % b, [P, N])
            nc.vector.tensor_scalar(result[:], centred[:], inverse[:], gk_cols[:, b:b + 1], ALU.mult, ALU.mult)
            nc.sync.dma_start(out_rows[b], result[:])

        acc = [sums.tile([P, N], F32, name="acc%d" % b) for b in range(BLOCKS)]

        over = sb("x_over0", [P, PASS])
        picked = at(B, "x_picked0", [P, PASS])
        gather_x(0, over, picked)
        for a in range(PASSES):
            spread(rb_row[a], rb_cols[:, a, :], 4, nc.scalar.copy)
        x_bank = turn_x1(0, picked)
        u_grouped0 = round_x0(0, over, at(A, "u_rounded00", [P, PASS], BF16))
        u_grouped1 = round_x1(0, x_bank)
        g_picked = [at(C, "g_picked00", [P, PASS]), sb("g_picked01", [P, PASS])]
        gather_g(0, 0, g_picked[0])
        gather_g(0, 1, g_picked[1])
        s_picked = [at(B, "s_picked00", [P, PASS])[:], at(A, "s_picked01", [P, PASS])[:]]
        for a in range(PASSES):
            gather_s(0, s_picked[a], entries(list_g, a))
        g_grouped0 = interleave(round_g(0, 0, g_picked[0], s_picked[0], at(C + W, "g_rounded00", [P, PASS], BF16)),
                                sb("g_grouped00", [P, PASS], BF16))
        quantise_u(0, 0, u_grouped0)
        quantise_u(0, 1, u_grouped1)
        g_next = [at(C, "g_picked10", [P, PASS]), at(C + W, "g_picked11", [P, PASS])]
        gather_g(1, 0, g_next[0])
        gather_g(1, 1, g_next[1])
        g_bank = round_g(0, 1, g_picked[1], s_picked[1], at(X0 + 64, "g_rounded01", [P, PASS], BF16))
        quantise_g(0, 0, g_grouped0)
        g_picked = g_next
        s_picked = [at(D, "s_picked10", [P, PASS])[:], at(G1, "s_picked11", [P, PASS])[:]]
        gather_s(1, s_picked[0], entries(list_g, 0))
        last = entries(list_g, 1)
        nc.vector.tensor_copy(s_picked[1][:, PASS // 2:], s_tab[1][:].indirect(last[:, LIST_COLS // 2:]))
        gather_s(1, s_picked[1][:, :PASS // 2], last[:, :LIST_COLS // 2])
        g_grouped1 = interleave(g_bank, at(S1, "g_grouped01", [P, PASS], BF16))
        g_banks = [round_g(1, a, g_picked[a], s_picked[a], sb("g_rounded1%d" % a, [P, PASS], BF16)) for a in range(PASSES)]
        quantise_g(0, 1, g_grouped1)
        over = at(C, "x_over1", [P, PASS])
        picked = at(D, "x_picked1", [P, PASS])
        gather_x(1, over, picked)
        x_bank = turn_x1(1, picked)
        g_grouped = [interleave(g_banks[a], at(X1 + a * W // 2, "g_grouped1%d" % a, [P, PASS], BF16)) for a in range(PASSES)]
        u_grouped0 = round_x0(1, over, sb("u_rounded10", [P, PASS], BF16))
        u_grouped1 = round_x1(1, x_bank)
        quantise_g(1, 1, g_grouped[1])
        quantise_g(1, 0, g_grouped[0])
        quantise_u(1, 1, u_grouped1)
        quantise_u(1, 0, u_grouped0)
        for b in range(BLOCKS):
            multiply(b, acc[b], 1)
            multiply(b, acc[b], 0)
        finish(0, acc[0])
        finish(1, acc[1])
